import numpy as np, ml_dtypes
CORES = [61,69,101,62,70,102]
N = 6
import mx_ref
NC, G = 256, 4
C = np.float32(0.037)
BF = ml_dtypes.bfloat16
def cut(t, i, w=512):
    return t[:, w * i:w * i + w]
def tile(rs):
    return np.stack(rs, axis=2).reshape(128, -1).astype(BF)
def layer(w, X):
    out = []
    for i in range(G):
        for t in range(len(X)):
            p = mx_ref.matmul(mx_ref.quantize(cut(w, len(X) * i + t)), X[t])
            z = p if t == 0 else z + p
        out.append(z)
    return out
def rot(Z, c, s):
    return [(Z[0] * c - Z[1] * s) * C, (Z[0] * s + Z[1] * c) * C, (Z[2] * c - Z[3] * s) * C, (Z[2] * s + Z[3] * c) * C]
def setup_inputs(rng):
    def f(*shape):
        return mx_ref.flush((rng.standard_normal(shape, dtype=np.float32) * np.exp2(rng.integers(-2, 3, shape[:-1] + (1,)))).astype(BF))
    ang = rng.random((N, 128, 128)) * (2 * np.pi)
    return {"cs": np.cos(ang).astype(BF), "sn": np.sin(ang).astype(BF), "xk": f(N, 128, 512), "wk": f(N, 128, G * 512), "xq": f(N, 128, 4 * NC)}
def setup_inputs_blocks(rng):
    d = setup_inputs(rng)
    for k in ("xk", "wk", "xq"): d[k] = mx_ref.spread(d[k], rng, 4)
    return d
def setup_inputs_wide(rng):
    d = setup_inputs(rng)
    for k in ("xk", "wk", "xq"): d[k] = mx_ref.flush((d[k].astype(np.float32) * np.exp2(rng.integers(-5, 6, (N, 1, 1))).astype(np.float32)).astype(BF))
    return d
def setup_inputs_zeros(rng):
    d = setup_inputs(rng); v = d["xk"].reshape(N, 128, -1, 4).copy()
    v[np.broadcast_to((rng.random((N, 1, v.shape[2], 1)) < 0.33), v.shape)] = 0
    d["xk"] = v.reshape(d["xk"].shape)
    return d
def reference(cs, sn, xk, wk, xq):
    K = [mx_ref.quantize(tile(rot(layer(wk[j], [mx_ref.quantize(xk[j])]), cs[j].astype(np.float32), sn[j].astype(np.float32)))) for j in range(N)]
    y = np.zeros((N, 128, N * NC), np.float32)
    for r in range(N):
        q = mx_ref.quantize(xq[r])
        for j in range(N):
            y[r][:, NC * j:NC * j + NC] = mx_ref.matmul(K[j], q)
    return {"y": y}

@@ -1,0 +1,249 @@
+import numpy as np
+from concourse.bass import DstId, RemoteDMATransfer
+from concourse.mybir import dt, AluOpType, ActivationFunctionType
+
+N = 6
+CPY = ActivationFunctionType.Copy
+F8 = "float8_e4m3fn_x4"
+SCRATCH = {
+    "xk_t": ("sbuf", [128, 512], "bfloat16"),
+    "wk_t": ("sbuf", [128, 2048], "bfloat16"),
+    "xq_t": ("sbuf", [128, 1024], "bfloat16"),
+    "c_t": ("sbuf", [128, 128], "bfloat16"),
+    "s_t": ("sbuf", [128, 128], "bfloat16"),
+    "xk_c": ("sbuf", [128, 128], F8),
+    "xk_s": ("sbuf", [128, 128], "uint8"),
+    "wk_c": ("sbuf", [128, 512], F8),
+    "wk_s": ("sbuf", [128, 512], "uint8"),
+    "xq_c": ("sbuf", [128, 256], F8),
+    "xq_s": ("sbuf", [128, 256], "uint8"),
+    "d0": ("sbuf", [128, 512], "float32"),
+    "d1": ("sbuf", [128, 1024], "float32"),
+    "ro": ("sbuf", [128, 1024], "float32"),
+    "k_t": ("sbuf", [128, 512], "bfloat16"),
+    "k_c": ("sbuf", [128, 128 * N], F8),
+    "k_s": ("sbuf", [128, 128 * N], "uint8"),
+    "yo": ("sbuf", [128, 256 * N], "float32"),
+    "z": ("psum", [128, 2048], "float32"),
+    "yp": ("psum", [128, 2048], "float32"),
+}
+SEMAPHORES = (["lx", "lwa", "lwb", "lc", "ls", "lq", "ms", "qx", "qw0", "qw1", "qw2", "qw3", "qq",
+               "m0", "m1", "m2", "m3", "prep", "zc0", "zc2", "p0", "p1", "p2", "p3",
+               "n0", "n1", "n2", "n3", "sc", "r3", "kq", "hs", "hc", "snt"]
+              + ["arr%d" % j for j in range(N)] + ["my%d" % j for j in range(N)]
+              + ["yc%d" % j for j in range(N)] + ["st%d" % j for j in range(N)])
+
+
+def _bits(m):
+    return [b for b in range(m.bit_length()) if (m >> b) & 1]
+
+
+def _alternate(m):
+    out = 0
+    for b in _bits(m)[::2]:
+        out |= 1 << b
+    return out
+
+
+def _plan(T, topo):
+    plan = {}
+    taken = set(T.cores)
+    for src in T.cores:
+        others = [d for d in T.cores if d != src]
+        near = [d for d in others if topo.chip(d) == topo.chip(src)]
+        off = [d for d in others if d not in near and topo.may_write(src, d)]
+        off.sort(key=lambda d: topo.same_plane(topo.chip(src), topo.chip(d)))
+        rest = [d for d in others if d not in near and d not in off]
+        helpers = {}
+        for ch in sorted(set(topo.chip(d) for d in rest)):
+            ds = [d for d in rest if topo.chip(d) == ch]
+            free = [8 * topo.chip(src) + k for k in range(8)]
+            free = [c for c in free if topo.chip(c) == topo.chip(src) and c not in taken
+                    and topo.die(c) != topo.die(src) and all(topo.may_write(c, d) for d in ds)]
+            h = free[0]
+            taken.add(h)
+            helpers[h] = ds
+        plan[src] = (near, off, helpers)
+    return plan
+
+
+def _masks(src, dsts, near_style, T, topo):
+    m = topo.mask(src, dsts[0])
+    for d in dsts:
+        m &= topo.mask(src, d)
+    if near_style == "alternate":
+        return _alternate(m)
+    if near_style == "rest":
+        for d in T.cores:
+            if topo.chip(d) != topo.chip(src):
+                m &= ~topo.mask(src, d)
+    return m
+
+
+def _spread(g, T, topo, src, j, dsts, style, what, sem, sent):
+    a, b = 128 * j, 128 * j + 128
+
+    def ap():
+        return T.k_s[:, a:b] if what == "s" else T.k_c[:, a:b].bitcast(dt.uint8)
+    m = _masks(src, dsts, style, T, topo)
+    ids = []
+    for d in dsts:
+        rid, pid, _e = topo.addr(d)
+        ids.append(DstId(rid=rid, pnc=pid))
+    g.remote_dma_fused([RemoteDMATransfer(dst_ids=ids, dma_engine_mask=m, remote_sem=sem, srcs=[ap()],
+                                          dsts=[ap() for _d in dsts])], local_sem=T.sem.snt)
+    sent[0] += len(_bits(m))
+
+
+def rank_program(g, core, T, topo):
+    plan = _plan(T, topo)
+    rank = T.rank_of(core)
+    sem = T.sem
+    sent = [0]
+    if rank is None:
+        for src in T.cores:
+            helpers = plan[src][2]
+            if core in helpers:
+                j = T.rank_of(src)
+                n = len(_bits(_masks(src, sorted(helpers), "alternate", T, topo)))
+                for what, s in (("s", sem.hs), ("c", sem.hc)):
+                    g.wait_ge(s, n)
+                    _spread(g, T, topo, core, j, helpers[core], "all", what, sem["arr%d" % j], sent)
+                g.wait_ge(sem.snt, sent[0])
+        return
+
+    near, off, helpers = plan[core]
+    V, S, P, Y = g.vector, g.scalar, g.tensor, g.sync
+    MUL, ADD, SUB = AluOpType.mult, AluOpType.add, AluOpType.subtract
+    C = float(np.float32(0.037))
+    own = slice(128 * rank, 128 * rank + 128)
+
+    need, via = {}, {}
+    for src in T.cores:
+        if src == core:
+            continue
+        j = T.rank_of(src)
+        s_near, s_off, s_help = plan[src]
+        if core in s_near:
+            m, via[j] = _masks(src, s_near, "rest", T, topo), 0
+        elif core in s_off:
+            m = _masks(src, s_off, "all", T, topo)
+            via[j] = 1 if topo.same_plane(topo.chip(src), topo.chip(core)) else 2
+        else:
+            h = [h for h in s_help if core in s_help[h]][0]
+            m, via[j] = _masks(h, s_help[h], "all", T, topo), 3
+        need[j] = 2 * len(_bits(m))
+    order = [rank] + sorted(need, key=lambda j: (via[j], j))
+
+    Y.dma_start(T.wk_t[:, 0:1024], T.wk[:, 0:1024]).then_inc(sem.lwa, 16)
+    Y.dma_start(T.wk_t[:, 1024:2048], T.wk[:, 1024:2048]).then_inc(sem.lwb, 16)
+    S.dma_start(T.xk_t[:], T.xk[:]).then_inc(sem.lx, 16)
+    S.dma_start(T.c_t[:], T.cs[:]).then_inc(sem.lc, 16)
+    S.dma_start(T.s_t[:], T.sn[:]).then_inc(sem.ls, 16)
+    Y.wait_ge(sem.lwb, 16)
+    Y.dma_start(T.xq_t[:], T.xq[:]).then_inc(sem.lq, 16)
+
+    def quant_w(i):
+        V.quantize_mx(T.wk_c[:, 128 * i:128 * i + 128], T.wk_s[:, 128 * i:128 * i + 128],
+                      T.wk_t[:, 512 * i:512 * i + 512]).then_inc(sem["qw%d" % i], 1)
+
+    def prod(b, zi, t):
+        V.tensor_tensor(T.d1[:, 256 * b + 1:256 * b + 256:2], T.z[:, 512 * zi:512 * zi + 128], t, MUL).then_inc(sem["p%d" % b], 1)
+
+    def scan(b):
+        V.wait_ge(sem["p%d" % b], 1)
+        h = 256 * (b // 2)
+        V.tensor_tensor_scan(T.ro[:, 256 * b:256 * b + 256], T.d0[:, h:h + 256], T.d1[:, 256 * b:256 * b + 256],
+                             0.0, MUL, ADD if b % 2 else SUB).then_inc(sem["n%d" % b], 1)
+
+    V.memset(T.d0[:], 0.0).then_inc(sem.ms, 1)
+    V.wait_ge(sem.lx, 16)
+    V.quantize_mx(T.xk_c[:], T.xk_s[:], T.xk_t[:]).then_inc(sem.qx, 1)
+    V.wait_ge(sem.lwa, 16)
+    quant_w(1)
+    quant_w(0)
+    V.wait_ge(sem.lc, 16)
+    V.wait_ge(sem.ls, 16)
+    V.wait_ge(sem.m1, 1)
+    prod(0, 1, T.s_t[:])
+    prod(1, 1, T.c_t[:])
+    V.wait_ge(sem.prep, 4)
+    V.wait_ge(sem.zc0, 1)
+    scan(0)
+    scan(1)
+    V.wait_ge(sem.lwb, 16)
+    quant_w(3)
+    quant_w(2)
+    V.wait_ge(sem.m3, 1)
+    prod(2, 3, T.s_t[:])
+    prod(3, 3, T.c_t[:])
+    V.wait_ge(sem.zc2, 1)
+    scan(2)
+    scan(3)
+    V.wait_ge(sem.n3, 1)
+    V.tensor_scalar(T.k_t[:, 3:512:4], T.ro[:, 769:1024:2], C, None, MUL).then_inc(sem.r3, 1)
+    V.wait_ge(sem.sc, 3)
+    V.wait_ge(sem.r3, 1)
+    V.quantize_mx(T.k_c[:, own], T.k_s[:, own], T.k_t[:]).then_inc(sem.kq, 1)
+    V.wait_ge(sem.lq, 16)
+    V.quantize_mx(T.xq_c[:], T.xq_s[:], T.xq_t[:]).then_inc(sem.qq, 1)
+
+    S.wait_ge(sem.lc, 16)
+    for b in (0, 2):
+        S.activation(T.d1[:, 256 * b:256 * b + 255:2], T.c_t[:], CPY, scale=-1.0).then_inc(sem.prep, 1)
+    S.wait_ge(sem.ls, 16)
+    for b in (1, 3):
+        S.activation(T.d1[:, 256 * b:256 * b + 255:2], T.s_t[:], CPY).then_inc(sem.prep, 1)
+    S.wait_ge(sem.ms, 1)
+
+    def z_copy(i):
+        S.wait_ge(sem["m%d" % i], 1)
+        S.activation(T.d0[:, 128 * i + 1:128 * i + 256:2], T.z[:, 512 * i:512 * i + 128], CPY).then_inc(sem["zc%d" % i], 1)
+
+    def scaled(b):
+        S.wait_ge(sem["n%d" % b], 1)
+        S.activation(T.k_t[:, b:512:4], T.ro[:, 256 * b + 1:256 * b + 256:2], CPY, scale=C).then_inc(sem.sc, 1)
+    z_copy(0)
+    scaled(0)
+    scaled(1)
+    z_copy(2)
+    scaled(2)
+
+    P.wait_ge(sem.qx, 1)
+    for i in (1, 0, 3, 2):
+        P.wait_ge(sem["qw%d" % i], 1)
+        P.matmul_mx(T.z[:, 512 * i:512 * i + 128], T.wk_c[:, 128 * i:128 * i + 128], T.wk_s[:, 128 * i:128 * i + 128],
+                    T.xk_c[:], T.xk_s[:], True, True).then_inc(sem["m%d" % i], 1)
+    P.wait_ge(sem.kq, 1)
+    P.wait_ge(sem.qq, 1)
+    for k, j in enumerate(order):
+        if j != rank:
+            P.wait_ge(sem["arr%d" % j], need[j])
+        bank = T.yp[:, 512 * k:512 * k + 256] if k < 4 else T.z[:, 512 * (k - 4):512 * (k - 4) + 256]
+        P.matmul_mx(bank, T.k_c[:, 128 * j:128 * j + 128], T.k_s[:, 128 * j:128 * j + 128],
+                    T.xq_c[:], T.xq_s[:], True, True).then_inc(sem["my%d" % j], 1)
+        cols = slice(256 * j, 256 * j + 256)
+        if k % 2:
+            V.wait_ge(sem["my%d" % j], 1)
+            V.tensor_copy(T.yo[:, cols], bank).then_inc(sem["yc%d" % j], 1)
+            q = Y
+        else:
+            S.wait_ge(sem["my%d" % j], 1)
+            S.activation(T.yo[:, cols], bank, CPY).then_inc(sem["yc%d" % j], 1)
+            q = S
+        q.wait_ge(sem["yc%d" % j], 1)
+        q.dma_start(T.y[:, cols], T.yo[:, cols]).then_inc(sem["st%d" % j], 16)
+    for j in order:
+        Y.wait_ge(sem["st%d" % j], 16)
+
+    g.wait_ge(sem.kq, 1)
+    arr = sem["arr%d" % rank]
+    if helpers:
+        for what, s in (("s", sem.hs), ("c", sem.hc)):
+            _spread(g, T, topo, core, rank, sorted(helpers), "alternate", what, s, sent)
+    if off:
+        for what in ("s", "c"):
+            _spread(g, T, topo, core, rank, off, "all", what, arr, sent)
+    for what in ("s", "c"):
+        _spread(g, T, topo, core, rank, near, "rest", what, arr, sent)
+    g.wait_ge(sem.snt, sent[0])

@@ -3,6 +3,7 @@ from concourse.bass import DstId, RemoteDMATransfer
 from concourse.mybir import dt, AluOpType, ActivationFunctionType
 
 N = 6
+CHIPS = 14
 CPY = ActivationFunctionType.Copy
 F8 = "float8_e4m3fn_x4"
 SCRATCH = {
@@ -27,120 +28,166 @@ SCRATCH = {
     "z": ("psum", [128, 2048], "float32"),
     "yp": ("psum", [128, 2048], "float32"),
 }
-SEMAPHORES = (["lx", "lwa", "lwb", "lc", "ls", "lq", "ms", "qx", "qw0", "qw1", "qw2", "qw3", "qq",
-               "m0", "m1", "m2", "m3", "prep", "zc0", "zc2", "p0", "p1", "p2", "p3",
-               "n0", "n1", "n2", "n3", "sc", "r3", "kq", "hs", "hc", "snt"]
-              + ["arr%d" % j for j in range(N)] + ["my%d" % j for j in range(N)]
-              + ["yc%d" % j for j in range(N)] + ["st%d" % j for j in range(N)])
+SEMAPHORES = (["lx", "lw01", "lw23", "lc", "ls", "lq", "ms", "qx", "qw0", "qw1", "qw2", "qw3", "qq",
+               "m0", "m1", "m2", "m3", "prepa", "prepb", "zc0", "zc2", "p0", "p1", "p2", "p3",
+               "n0", "n1", "n2", "n3", "sc", "r3", "kq", "snt"]
+              + ["as%d" % j for j in range(N)] + ["ac%d" % j for j in range(N)]
+              + ["my%d" % i for i in range(N)] + ["yc%d" % i for i in range(N)] + ["st%d" % i for i in range(N)])
 
 
 def _bits(m):
     return [b for b in range(m.bit_length()) if (m >> b) & 1]
 
 
-def _alternate(m):
-    out = 0
-    for b in _bits(m)[::2]:
-        out |= 1 << b
-    return out
-
-
-def _plan(T, topo):
-    plan = {}
-    taken = set(T.cores)
-    for src in T.cores:
-        others = [d for d in T.cores if d != src]
-        near = [d for d in others if topo.chip(d) == topo.chip(src)]
-        off = [d for d in others if d not in near and topo.may_write(src, d)]
-        off.sort(key=lambda d: topo.same_plane(topo.chip(src), topo.chip(d)))
-        rest = [d for d in others if d not in near and d not in off]
-        helpers = {}
-        for ch in sorted(set(topo.chip(d) for d in rest)):
-            ds = [d for d in rest if topo.chip(d) == ch]
-            free = [8 * topo.chip(src) + k for k in range(8)]
-            free = [c for c in free if topo.chip(c) == topo.chip(src) and c not in taken
-                    and topo.die(c) != topo.die(src) and all(topo.may_write(c, d) for d in ds)]
-            h = free[0]
-            taken.add(h)
-            helpers[h] = ds
-        plan[src] = (near, off, helpers)
-    return plan
-
-
-def _masks(src, dsts, near_style, T, topo):
+def _common(src, dsts, topo):
     m = topo.mask(src, dsts[0])
     for d in dsts:
         m &= topo.mask(src, d)
-    if near_style == "alternate":
-        return _alternate(m)
-    if near_style == "rest":
-        for d in T.cores:
-            if topo.chip(d) != topo.chip(src):
-                m &= ~topo.mask(src, d)
     return m
 
 
-def _spread(g, T, topo, src, j, dsts, style, what, sem, sent):
-    a, b = 128 * j, 128 * j + 128
+def _plan(T, topo):
+    chips = sorted(set(topo.chip(c) for c in T.cores))
+    members = {ch: sorted((c for c in T.cores if topo.chip(c) == ch), key=T.rank_of) for ch in chips}
+    order = [T.rank_of(c) for ch in chips for c in members[ch]]
+    slot = {j: order.index(j) for j in order}
+    taken = set(T.cores)
+    calls, forwards, landed = [], [], {}
 
-    def ap():
-        return T.k_s[:, a:b] if what == "s" else T.k_c[:, a:b].bitcast(dt.uint8)
-    m = _masks(src, dsts, style, T, topo)
-    ids = []
-    for d in dsts:
-        rid, pid, _e = topo.addr(d)
-        ids.append(DstId(rid=rid, pnc=pid))
-    g.remote_dma_fused([RemoteDMATransfer(dst_ids=ids, dma_engine_mask=m, remote_sem=sem, srcs=[ap()],
-                                          dsts=[ap() for _d in dsts])], local_sem=T.sem.snt)
-    sent[0] += len(_bits(m))
+    def reach(c, dsts):
+        return all(topo.may_write(c, d) for d in dsts)
+
+    def free(ch, die, dsts):
+        for one in (die, 1 - die):
+            for c in range(8 * ch, 8 * ch + 8):
+                if c not in taken and topo.die(c) == one and reach(c, dsts):
+                    taken.add(c)
+                    return c
+        return None
+
+    for ch in chips:
+        me = members[ch]
+        ranks = [T.rank_of(c) for c in me]
+        other = [c2 for c2 in chips if c2 != ch]
+        direct = {}
+        for src in me:
+            ok = [c2 for c2 in other if reach(src, members[c2])]
+            ok.sort(key=lambda c2: (c2 in direct.values(), topo.same_plane(ch, c2), -c2))
+            if ok:
+                direct[src] = ok[0]
+        left = [c2 for c2 in other if c2 not in direct.values()]
+        legs = [(src, c2) for src in me for c2 in other if direct.get(src) != c2]
+        first, second = {}, {}
+        for src, c2 in legs:
+            first[(src, c2)] = free(ch, topo.die(src) if c2 in left else 1 - topo.die(src), members[c2])
+        for src, c2 in sorted(legs, key=lambda t: not topo.same_plane(ch, t[1])):
+            die = 1 - topo.die(first[(src, c2)])
+            c = free(ch, die, members[c2]) if not left else None
+            for x in range(CHIPS):
+                if c is None and topo.mates(x, c2) and topo.same_plane(x, ch):
+                    c = free(x, die, members[c2])
+            second[(src, c2)] = c
+        pairs = {c2: first[(me[0], c2)] for c2 in left}
+        for src in me:
+            j = T.rank_of(src)
+            near = [c for c in me if c != src]
+            off = [d for c2 in other for d in members[c2]]
+            low = _common(src, off, topo)
+            upper = _common(src, near, topo) & ~low
+            here = ([first[t] for t in legs if t[0] == src]
+                    + [second[t] for t in legs if t[0] == src and topo.chip(second[t]) == ch])
+            away = [second[t] for t in legs if t[0] == src and topo.chip(second[t]) != ch]
+            if src in direct:
+                ds = members[direct[src]]
+                n = landed.get(direct[src], 0)
+                landed[direct[src]] = n + 1
+                at = ds[n % len(ds)]
+                away = away + [at]
+                rest = [d for d in ds if d != at]
+                forwards.append((at, "c", [j], rest, _common(at, rest, topo)))
+            calls.append((src, "s", [j], near + sorted(pairs.values()), upper))
+            calls.append((src, "c", [j], here, upper))
+            calls.append((src, "c", [j], away, low))
+            calls.append((src, "c", [j], near, _common(src, near, topo)))
+            if src in direct:
+                calls.append((src, "s", ranks, ds, low))
+        for c2 in left:
+            calls.append((pairs[c2], "s", ranks, members[c2], _common(pairs[c2], members[c2], topo)))
+        for t in legs:
+            ds = members[t[1]]
+            for h, d in ((first[t], ds[0]), (second[t], ds[1])):
+                calls.append((h, "c", [T.rank_of(t[0])], [d], _common(h, [d], topo)))
+    return calls + forwards, slot
 
 
 def rank_program(g, core, T, topo):
-    plan = _plan(T, topo)
+    calls, slot = _plan(T, topo)
     rank = T.rank_of(core)
     sem = T.sem
-    sent = [0]
-    if rank is None:
-        for src in T.cores:
-            helpers = plan[src][2]
-            if core in helpers:
-                j = T.rank_of(src)
-                n = len(_bits(_masks(src, sorted(helpers), "alternate", T, topo)))
-                for what, s in (("s", sem.hs), ("c", sem.hc)):
-                    g.wait_ge(s, n)
-                    _spread(g, T, topo, core, j, helpers[core], "all", what, sem["arr%d" % j], sent)
-                g.wait_ge(sem.snt, sent[0])
+    mine = [c for c in calls if c[0] == core]
+    arrive = {}
+    via = {}
+    for (src, what, js, dsts, m) in calls:
+        if core in dsts:
+            for j in js:
+                if j != rank:
+                    arrive[(what, j)] = (sem["a%s%d" % (what, js[0])], len(_bits(m)))
+                    via[(what, j)] = src
+    if not mine and not arrive:
         return
 
-    near, off, helpers = plan[core]
+    def send_all():
+        sent, waited = 0, set()
+        for (_src, what, js, dsts, m) in mine:
+            for j in js:
+                if j == rank:
+                    if j not in waited:
+                        g.wait_ge(sem.kq, 1)
+                        waited.add(j)
+                elif (what, j) not in waited:
+                    g.wait_ge(*arrive[(what, j)])
+                    waited.add((what, j))
+            a, b = 128 * slot[js[0]], 128 * slot[js[-1]] + 128
+
+            def ap():
+                return T.k_s[:, a:b] if what == "s" else T.k_c[:, a:b].bitcast(dt.uint8)
+            ids = []
+            for d in dsts:
+                rid, pid, _e = topo.addr(d)
+                ids.append(DstId(rid=rid, pnc=pid))
+            g.remote_dma_fused([RemoteDMATransfer(dst_ids=ids, dma_engine_mask=m, remote_sem=sem["a%s%d" % (what, js[0])],
+                                                  srcs=[ap()], dsts=[ap() for _d in dsts])], local_sem=sem.snt)
+            sent += len(_bits(m))
+        g.wait_ge(sem.snt, sent)
+
+    if rank is None:
+        send_all()
+        return
+
     V, S, P, Y = g.vector, g.scalar, g.tensor, g.sync
     MUL, ADD, SUB = AluOpType.mult, AluOpType.add, AluOpType.subtract
     C = float(np.float32(0.037))
-    own = slice(128 * rank, 128 * rank + 128)
+    own = slice(128 * slot[rank], 128 * slot[rank] + 128)
 
-    need, via = {}, {}
-    for src in T.cores:
-        if src == core:
-            continue
-        j = T.rank_of(src)
-        s_near, s_off, s_help = plan[src]
-        if core in s_near:
-            m, via[j] = _masks(src, s_near, "rest", T, topo), 0
-        elif core in s_off:
-            m = _masks(src, s_off, "all", T, topo)
-            via[j] = 1 if topo.same_plane(topo.chip(src), topo.chip(core)) else 2
-        else:
-            h = [h for h in s_help if core in s_help[h]][0]
-            m, via[j] = _masks(h, s_help[h], "all", T, topo), 3
-        need[j] = 2 * len(_bits(m))
-    order = [rank] + sorted(need, key=lambda j: (via[j], j))
+    def when(j):
+        if j == rank:
+            return (0,)
+        src = via[("c", j)]
+        if src == T.cores[j]:
+            return (1, 0) if topo.chip(src) == topo.chip(core) else (2, 0)
+        if T.rank_of(src) is not None:
+            return (3, 0)
+        home = T.cores[j]
+        far = [d for d in T.cores if topo.chip(d) != topo.chip(home)]
+        return (4, not any(topo.may_write(home, d) for d in far), not topo.same_plane(topo.chip(home), topo.chip(core)), j)
+    order = sorted(range(N), key=when)
 
-    Y.dma_start(T.wk_t[:, 0:1024], T.wk[:, 0:1024]).then_inc(sem.lwa, 16)
-    Y.dma_start(T.wk_t[:, 1024:2048], T.wk[:, 1024:2048]).then_inc(sem.lwb, 16)
+    Y.dma_start(T.wk_t[:, 0:1024], T.wk[:, 0:1024]).then_inc(sem.lw01, 16)
     S.dma_start(T.xk_t[:], T.xk[:]).then_inc(sem.lx, 16)
     S.dma_start(T.c_t[:], T.cs[:]).then_inc(sem.lc, 16)
-    S.dma_start(T.s_t[:], T.sn[:]).then_inc(sem.ls, 16)
-    Y.wait_ge(sem.lwb, 16)
+    Y.dma_start(T.s_t[:], T.sn[:]).then_inc(sem.ls, 16)
+    Y.dma_start(T.wk_t[:, 1024:2048], T.wk[:, 1024:2048]).then_inc(sem.lw23, 16)
+    Y.wait_ge(sem.lw23, 16)
     Y.dma_start(T.xq_t[:], T.xq[:]).then_inc(sem.lq, 16)
 
     def quant_w(i):
@@ -159,7 +206,7 @@ def rank_program(g, core, T, topo):
     V.memset(T.d0[:], 0.0).then_inc(sem.ms, 1)
     V.wait_ge(sem.lx, 16)
     V.quantize_mx(T.xk_c[:], T.xk_s[:], T.xk_t[:]).then_inc(sem.qx, 1)
-    V.wait_ge(sem.lwa, 16)
+    V.wait_ge(sem.lw01, 16)
     quant_w(1)
     quant_w(0)
     V.wait_ge(sem.lc, 16)
@@ -167,16 +214,17 @@ def rank_program(g, core, T, topo):
     V.wait_ge(sem.m1, 1)
     prod(0, 1, T.s_t[:])
     prod(1, 1, T.c_t[:])
-    V.wait_ge(sem.prep, 4)
+    V.wait_ge(sem.prepa, 2)
     V.wait_ge(sem.zc0, 1)
     scan(0)
-    scan(1)
-    V.wait_ge(sem.lwb, 16)
+    V.wait_ge(sem.lw23, 16)
     quant_w(3)
     quant_w(2)
+    scan(1)
     V.wait_ge(sem.m3, 1)
     prod(2, 3, T.s_t[:])
     prod(3, 3, T.c_t[:])
+    V.wait_ge(sem.prepb, 2)
     V.wait_ge(sem.zc2, 1)
     scan(2)
     scan(3)
@@ -188,13 +236,13 @@ def rank_program(g, core, T, topo):
     V.wait_ge(sem.lq, 16)
     V.quantize_mx(T.xq_c[:], T.xq_s[:], T.xq_t[:]).then_inc(sem.qq, 1)
 
-    S.wait_ge(sem.lc, 16)
-    for b in (0, 2):
-        S.activation(T.d1[:, 256 * b:256 * b + 255:2], T.c_t[:], CPY, scale=-1.0).then_inc(sem.prep, 1)
-    S.wait_ge(sem.ls, 16)
-    for b in (1, 3):
-        S.activation(T.d1[:, 256 * b:256 * b + 255:2], T.s_t[:], CPY).then_inc(sem.prep, 1)
-    S.wait_ge(sem.ms, 1)
+    def prep(b):
+        into = T.d1[:, 256 * b:256 * b + 255:2]
+        done = sem.prepb if b // 2 else sem.prepa
+        if b % 2:
+            S.activation(into, T.s_t[:], CPY).then_inc(done, 1)
+        else:
+            S.activation(into, T.c_t[:], CPY, scale=-1.0).then_inc(done, 1)
 
     def z_copy(i):
         S.wait_ge(sem["m%d" % i], 1)
@@ -203,10 +251,17 @@ def rank_program(g, core, T, topo):
     def scaled(b):
         S.wait_ge(sem["n%d" % b], 1)
         S.activation(T.k_t[:, b:512:4], T.ro[:, 256 * b + 1:256 * b + 256:2], CPY, scale=C).then_inc(sem.sc, 1)
+    S.wait_ge(sem.lc, 16)
+    prep(0)
+    S.wait_ge(sem.ls, 16)
+    prep(1)
+    S.wait_ge(sem.ms, 1)
     z_copy(0)
+    prep(2)
+    prep(3)
     scaled(0)
-    scaled(1)
     z_copy(2)
+    scaled(1)
     scaled(2)
 
     P.wait_ge(sem.qx, 1)
@@ -218,32 +273,24 @@ def rank_program(g, core, T, topo):
     P.wait_ge(sem.qq, 1)
     for k, j in enumerate(order):
         if j != rank:
-            P.wait_ge(sem["arr%d" % j], need[j])
-        bank = T.yp[:, 512 * k:512 * k + 256] if k < 4 else T.z[:, 512 * (k - 4):512 * (k - 4) + 256]
-        P.matmul_mx(bank, T.k_c[:, 128 * j:128 * j + 128], T.k_s[:, 128 * j:128 * j + 128],
-                    T.xq_c[:], T.xq_s[:], True, True).then_inc(sem["my%d" % j], 1)
+            P.wait_ge(*arrive[("s", j)])
+            P.wait_ge(*arrive[("c", j)])
+        at = 512 * (k % 4)
+        bank = (T.yp if k < 4 else T.z)[:, at:at + 256]
+        tile = slice(128 * slot[j], 128 * slot[j] + 128)
+        P.matmul_mx(bank, T.k_c[:, tile], T.k_s[:, tile], T.xq_c[:], T.xq_s[:], True, True).then_inc(sem["my%d" % k], 1)
         cols = slice(256 * j, 256 * j + 256)
         if k % 2:
-            V.wait_ge(sem["my%d" % j], 1)
-            V.tensor_copy(T.yo[:, cols], bank).then_inc(sem["yc%d" % j], 1)
+            V.wait_ge(sem["my%d" % k], 1)
+            V.tensor_copy(T.yo[:, cols], bank).then_inc(sem["yc%d" % k], 1)
             q = Y
         else:
-            S.wait_ge(sem["my%d" % j], 1)
-            S.activation(T.yo[:, cols], bank, CPY).then_inc(sem["yc%d" % j], 1)
+            S.wait_ge(sem["my%d" % k], 1)
+            S.activation(T.yo[:, cols], bank, CPY).then_inc(sem["yc%d" % k], 1)
             q = S
-        q.wait_ge(sem["yc%d" % j], 1)
-        q.dma_start(T.y[:, cols], T.yo[:, cols]).then_inc(sem["st%d" % j], 16)
-    for j in order:
-        Y.wait_ge(sem["st%d" % j], 16)
+        q.wait_ge(sem["yc%d" % k], 1)
+        q.dma_start(T.y[:, cols], T.yo[:, cols]).then_inc(sem["st%d" % k], 16)
+    for k in range(N):
+        Y.wait_ge(sem["st%d" % k], 16)
 
-    g.wait_ge(sem.kq, 1)
-    arr = sem["arr%d" % rank]
-    if helpers:
-        for what, s in (("s", sem.hs), ("c", sem.hc)):
-            _spread(g, T, topo, core, rank, sorted(helpers), "alternate", what, s, sent)
-    if off:
-        for what in ("s", "c"):
-            _spread(g, T, topo, core, rank, off, "all", what, arr, sent)
-    for what in ("s", "c"):
-        _spread(g, T, topo, core, rank, near, "rest", what, arr, sent)
-    g.wait_ge(sem.snt, sent[0])
+    send_all()

import numpy as np
from concourse.bass import DstId, RemoteDMATransfer
from concourse.mybir import dt, AluOpType, ActivationFunctionType

N = 6
CHIPS = 14
CPY = ActivationFunctionType.Copy
F8 = "float8_e4m3fn_x4"
SCRATCH = {
    "xk_t": ("sbuf", [128, 512], "bfloat16"),
    "wk_t": ("sbuf", [128, 2048], "bfloat16"),
    "xq_t": ("sbuf", [128, 1024], "bfloat16"),
    "c_t": ("sbuf", [128, 128], "bfloat16"),
    "s_t": ("sbuf", [128, 128], "bfloat16"),
    "xk_c": ("sbuf", [128, 128], F8),
    "xk_s": ("sbuf", [128, 128], "uint8"),
    "wk_c": ("sbuf", [128, 512], F8),
    "wk_s": ("sbuf", [128, 512], "uint8"),
    "xq_c": ("sbuf", [128, 256], F8),
    "xq_s": ("sbuf", [128, 256], "uint8"),
    "d0": ("sbuf", [128, 512], "float32"),
    "d1": ("sbuf", [128, 1024], "float32"),
    "ro": ("sbuf", [128, 1024], "float32"),
    "k_t": ("sbuf", [128, 512], "bfloat16"),
    "k_c": ("sbuf", [128, 128 * N], F8),
    "k_s": ("sbuf", [128, 128 * N], "uint8"),
    "yo": ("sbuf", [128, 256 * N], "float32"),
    "z": ("psum", [128, 2048], "float32"),
    "yp": ("psum", [128, 2048], "float32"),
}
SEMAPHORES = (["lx", "lw01", "lw23", "lc", "ls", "lq", "ms", "qx", "qw0", "qw1", "qw2", "qw3", "qq",
               "m0", "m1", "m2", "m3", "prepa", "prepb", "zc0", "zc2", "p0", "p1", "p2", "p3",
               "n0", "n1", "n2", "n3", "sc", "r3", "kq", "snt"]
              + ["as%d" % j for j in range(N)] + ["ac%d" % j for j in range(N)]
              + ["my%d" % i for i in range(N)] + ["yc%d" % i for i in range(N)] + ["st%d" % i for i in range(N)])


def _bits(m):
    return [b for b in range(m.bit_length()) if (m >> b) & 1]


def _common(src, dsts, topo):
    m = topo.mask(src, dsts[0])
    for d in dsts:
        m &= topo.mask(src, d)
    return m


def _plan(T, topo):
    chips = sorted(set(topo.chip(c) for c in T.cores))
    members = {ch: sorted((c for c in T.cores if topo.chip(c) == ch), key=T.rank_of) for ch in chips}
    order = [T.rank_of(c) for ch in chips for c in members[ch]]
    slot = {j: order.index(j) for j in order}
    taken = set(T.cores)
    calls, forwards, landed = [], [], {}

    def reach(c, dsts):
        return all(topo.may_write(c, d) for d in dsts)

    def free(ch, die, dsts):
        for one in (die, 1 - die):
            for c in range(8 * ch, 8 * ch + 8):
                if c not in taken and topo.die(c) == one and reach(c, dsts):
                    taken.add(c)
                    return c
        return None

    for ch in chips:
        me = members[ch]
        ranks = [T.rank_of(c) for c in me]
        other = [c2 for c2 in chips if c2 != ch]
        direct = {}
        for src in me:
            ok = [c2 for c2 in other if reach(src, members[c2])]
            ok.sort(key=lambda c2: (c2 in direct.values(), topo.same_plane(ch, c2), -c2))
            if ok:
                direct[src] = ok[0]
        left = [c2 for c2 in other if c2 not in direct.values()]
        legs = [(src, c2) for src in me for c2 in other if direct.get(src) != c2]
        first, second = {}, {}
        for src, c2 in legs:
            first[(src, c2)] = free(ch, topo.die(src) if c2 in left else 1 - topo.die(src), members[c2])
        for src, c2 in sorted(legs, key=lambda t: not topo.same_plane(ch, t[1])):
            die = 1 - topo.die(first[(src, c2)])
            c = free(ch, die, members[c2]) if not left else None
            for x in range(CHIPS):
                if c is None and topo.mates(x, c2) and topo.same_plane(x, ch):
                    c = free(x, die, members[c2])
            second[(src, c2)] = c
        pairs = {c2: first[(me[0], c2)] for c2 in left}
        for src in me:
            j = T.rank_of(src)
            near = [c for c in me if c != src]
            off = [d for c2 in other for d in members[c2]]
            low = _common(src, off, topo)
            upper = _common(src, near, topo) & ~low
            here = ([first[t] for t in legs if t[0] == src]
                    + [second[t] for t in legs if t[0] == src and topo.chip(second[t]) == ch])
            away = [second[t] for t in legs if t[0] == src and topo.chip(second[t]) != ch]
            if src in direct:
                ds = members[direct[src]]
                n = landed.get(direct[src], 0)
                landed[direct[src]] = n + 1
                at = ds[n % len(ds)]
                away = away + [at]
                rest = [d for d in ds if d != at]
                forwards.append((at, "c", [j], rest, _common(at, rest, topo)))
            calls.append((src, "s", [j], near + sorted(pairs.values()), upper))
            calls.append((src, "c", [j], here, upper))
            calls.append((src, "c", [j], away, low))
            calls.append((src, "c", [j], near, _common(src, near, topo)))
            if src in direct:
                calls.append((src, "s", ranks, ds, low))
        for c2 in left:
            calls.append((pairs[c2], "s", ranks, members[c2], _common(pairs[c2], members[c2], topo)))
        for t in legs:
            ds = members[t[1]]
            for h, d in ((first[t], ds[0]), (second[t], ds[1])):
                calls.append((h, "c", [T.rank_of(t[0])], [d], _common(h, [d], topo)))
    return calls + forwards, slot


def rank_program(g, core, T, topo):
    calls, slot = _plan(T, topo)
    rank = T.rank_of(core)
    sem = T.sem
    mine = [c for c in calls if c[0] == core]
    arrive = {}
    via = {}
    for (src, what, js, dsts, m) in calls:
        if core in dsts:
            for j in js:
                if j != rank:
                    arrive[(what, j)] = (sem["a%s%d" % (what, js[0])], len(_bits(m)))
                    via[(what, j)] = src
    if not mine and not arrive:
        return

    def send_all():
        sent, waited = 0, set()
        for (_src, what, js, dsts, m) in mine:
            for j in js:
                if j == rank:
                    if j not in waited:
                        g.wait_ge(sem.kq, 1)
                        waited.add(j)
                elif (what, j) not in waited:
                    g.wait_ge(*arrive[(what, j)])
                    waited.add((what, j))
            a, b = 128 * slot[js[0]], 128 * slot[js[-1]] + 128

            def ap():
                return T.k_s[:, a:b] if what == "s" else T.k_c[:, a:b].bitcast(dt.uint8)
            ids = []
            for d in dsts:
                rid, pid, _e = topo.addr(d)
                ids.append(DstId(rid=rid, pnc=pid))
            g.remote_dma_fused([RemoteDMATransfer(dst_ids=ids, dma_engine_mask=m, remote_sem=sem["a%s%d" % (what, js[0])],
                                                  srcs=[ap()], dsts=[ap() for _d in dsts])], local_sem=sem.snt)
            sent += len(_bits(m))
        g.wait_ge(sem.snt, sent)

    if rank is None:
        send_all()
        return

    V, S, P, Y = g.vector, g.scalar, g.tensor, g.sync
    MUL, ADD, SUB = AluOpType.mult, AluOpType.add, AluOpType.subtract
    C = float(np.float32(0.037))
    own = slice(128 * slot[rank], 128 * slot[rank] + 128)

    def when(j):
        if j == rank:
            return (0,)
        src = via[("c", j)]
        if src == T.cores[j]:
            return (1, 0) if topo.chip(src) == topo.chip(core) else (2, 0)
        if T.rank_of(src) is not None:
            return (3, 0)
        home = T.cores[j]
        far = [d for d in T.cores if topo.chip(d) != topo.chip(home)]
        return (4, not any(topo.may_write(home, d) for d in far), not topo.same_plane(topo.chip(home), topo.chip(core)), j)
    order = sorted(range(N), key=when)

    Y.dma_start(T.wk_t[:, 0:1024], T.wk[:, 0:1024]).then_inc(sem.lw01, 16)
    S.dma_start(T.xk_t[:], T.xk[:]).then_inc(sem.lx, 16)
    S.dma_start(T.c_t[:], T.cs[:]).then_inc(sem.lc, 16)
    Y.dma_start(T.s_t[:], T.sn[:]).then_inc(sem.ls, 16)
    Y.dma_start(T.wk_t[:, 1024:2048], T.wk[:, 1024:2048]).then_inc(sem.lw23, 16)
    Y.wait_ge(sem.lw23, 16)
    Y.dma_start(T.xq_t[:], T.xq[:]).then_inc(sem.lq, 16)

    def quant_w(i):
        V.quantize_mx(T.wk_c[:, 128 * i:128 * i + 128], T.wk_s[:, 128 * i:128 * i + 128],
                      T.wk_t[:, 512 * i:512 * i + 512]).then_inc(sem["qw%d" % i], 1)

    def prod(b, zi, t):
        V.tensor_tensor(T.d1[:, 256 * b + 1:256 * b + 256:2], T.z[:, 512 * zi:512 * zi + 128], t, MUL).then_inc(sem["p%d" % b], 1)

    def scan(b):
        V.wait_ge(sem["p%d" % b], 1)
        h = 256 * (b // 2)
        V.tensor_tensor_scan(T.ro[:, 256 * b:256 * b + 256], T.d0[:, h:h + 256], T.d1[:, 256 * b:256 * b + 256],
                             0.0, MUL, ADD if b % 2 else SUB).then_inc(sem["n%d" % b], 1)

    V.memset(T.d0[:], 0.0).then_inc(sem.ms, 1)
    V.wait_ge(sem.lx, 16)
    V.quantize_mx(T.xk_c[:], T.xk_s[:], T.xk_t[:]).then_inc(sem.qx, 1)
    V.wait_ge(sem.lw01, 16)
    quant_w(1)
    quant_w(0)
    V.wait_ge(sem.lc, 16)
    V.wait_ge(sem.ls, 16)
    V.wait_ge(sem.m1, 1)
    prod(0, 1, T.s_t[:])
    prod(1, 1, T.c_t[:])
    V.wait_ge(sem.prepa, 2)
    V.wait_ge(sem.zc0, 1)
    scan(0)
    V.wait_ge(sem.lw23, 16)
    quant_w(3)
    quant_w(2)
    scan(1)
    V.wait_ge(sem.m3, 1)
    prod(2, 3, T.s_t[:])
    prod(3, 3, T.c_t[:])
    V.wait_ge(sem.prepb, 2)
    V.wait_ge(sem.zc2, 1)
    scan(2)
    scan(3)
    V.wait_ge(sem.n3, 1)
    V.tensor_scalar(T.k_t[:, 3:512:4], T.ro[:, 769:1024:2], C, None, MUL).then_inc(sem.r3, 1)
    V.wait_ge(sem.sc, 3)
    V.wait_ge(sem.r3, 1)
    V.quantize_mx(T.k_c[:, own], T.k_s[:, own], T.k_t[:]).then_inc(sem.kq, 1)
    V.wait_ge(sem.lq, 16)
    V.quantize_mx(T.xq_c[:], T.xq_s[:], T.xq_t[:]).then_inc(sem.qq, 1)

    def prep(b):
        into = T.d1[:, 256 * b:256 * b + 255:2]
        done = sem.prepb if b // 2 else sem.prepa
        if b % 2:
            S.activation(into, T.s_t[:], CPY).then_inc(done, 1)
        else:
            S.activation(into, T.c_t[:], CPY, scale=-1.0).then_inc(done, 1)

    def z_copy(i):
        S.wait_ge(sem["m%d" % i], 1)
        S.activation(T.d0[:, 128 * i + 1:128 * i + 256:2], T.z[:, 512 * i:512 * i + 128], CPY).then_inc(sem["zc%d" % i], 1)

    def scaled(b):
        S.wait_ge(sem["n%d" % b], 1)
        S.activation(T.k_t[:, b:512:4], T.ro[:, 256 * b + 1:256 * b + 256:2], CPY, scale=C).then_inc(sem.sc, 1)
    S.wait_ge(sem.lc, 16)
    prep(0)
    S.wait_ge(sem.ls, 16)
    prep(1)
    S.wait_ge(sem.ms, 1)
    z_copy(0)
    prep(2)
    prep(3)
    scaled(0)
    z_copy(2)
    scaled(1)
    scaled(2)

    P.wait_ge(sem.qx, 1)
    for i in (1, 0, 3, 2):
        P.wait_ge(sem["qw%d" % i], 1)
        P.matmul_mx(T.z[:, 512 * i:512 * i + 128], T.wk_c[:, 128 * i:128 * i + 128], T.wk_s[:, 128 * i:128 * i + 128],
                    T.xk_c[:], T.xk_s[:], True, True).then_inc(sem["m%d" % i], 1)
    P.wait_ge(sem.kq, 1)
    P.wait_ge(sem.qq, 1)
    for k, j in enumerate(order):
        if j != rank:
            P.wait_ge(*arrive[("s", j)])
            P.wait_ge(*arrive[("c", j)])
        at = 512 * (k % 4)
        bank = (T.yp if k < 4 else T.z)[:, at:at + 256]
        tile = slice(128 * slot[j], 128 * slot[j] + 128)
        P.matmul_mx(bank, T.k_c[:, tile], T.k_s[:, tile], T.xq_c[:], T.xq_s[:], True, True).then_inc(sem["my%d" % k], 1)
        cols = slice(256 * j, 256 * j + 256)
        if k % 2:
            V.wait_ge(sem["my%d" % k], 1)
            V.tensor_copy(T.yo[:, cols], bank).then_inc(sem["yc%d" % k], 1)
            q = Y
        else:
            S.wait_ge(sem["my%d" % k], 1)
            S.activation(T.yo[:, cols], bank, CPY).then_inc(sem["yc%d" % k], 1)
            q = S
        q.wait_ge(sem["yc%d" % k], 1)
        q.dma_start(T.y[:, cols], T.yo[:, cols]).then_inc(sem["st%d" % k], 16)
    for k in range(N):
        Y.wait_ge(sem["st%d" % k], 16)

    send_all()
